import numpy as np
import ml_dtypes


def mxq(x, axis, fmt="e4m3"):
    dtype, down = {"e4m3": (ml_dtypes.float8_e4m3fn, 7), "e5m2": (ml_dtypes.float8_e5m2, 14)}[fmt]
    v = np.moveaxis(np.asarray(x, np.float32).astype(ml_dtypes.bfloat16).astype(np.float64), axis, -1)
    blocks = v.reshape(v.shape[:-1] + (-1, 32))
    amax = np.abs(blocks).max(-1, keepdims=True)
    byte = np.maximum(np.where(amax > 0, np.frexp(amax)[1] - 1 + 127, 0) - down, 1)
    scale = np.exp2(byte - 127.0)
    codes = (blocks / scale).astype(np.float32).astype(dtype).astype(np.float64)
    return np.moveaxis((codes * scale).reshape(v.shape), -1, axis)


WIDE = False


def mx_kscale(k):
    if not WIDE:
        return np.ones(k)
    levels = np.array([10, -10, 5, -5, 0])
    if k % 512:
        return np.exp2(np.random.permutation(np.resize(levels, k // 32))).repeat(32)
    a = np.empty((k // 512, 16))
    for p in range(k // 512):
        a[p, :8] = np.random.permutation(np.resize(levels, 8))
        for g in range(8):
            far = levels[np.abs(levels - a[p, g]) >= 10]
            a[p, g + 8] = far[np.random.randint(len(far))]
    return np.exp2(a.ravel()).repeat(32)


def f64(x):
    return np.asarray(x).astype(np.float64)


def striped(idx):
    return np.tile(idx.reshape(-1, 16).T, (8, 1)).astype(np.uint16)


def unstriped(offs):
    return offs[:16].T.reshape(-1).astype(np.int64)


E2M1 = np.array([0.0, 0.5, 1.0, 1.5, 2.0, 3.0, 4.0, 6.0, -0.0, -0.5, -1.0, -1.5, -2.0, -3.0, -4.0, -6.0])


def pack_weight(w, fmt):
    k, n = w.shape
    w = f64(np.asarray(w, np.float32).astype(ml_dtypes.bfloat16)).reshape(k // 32, 32, n)
    amax = np.abs(w).max(1)
    if fmt == "e4m3":
        byte = np.frexp(amax)[1] - 1 + 127 - 7
    else:
        mant, ex = np.frexp(amax / 6.0)
        byte = np.where(mant > 0.5, ex, ex - 1) + 127
    byte = np.clip(np.where(amax > 0, byte, 1), 1, 254)
    scaled = (w * np.exp2(127.0 - byte)[:, None, :]).reshape(k, n).astype(np.float32)
    by_word = np.ascontiguousarray(scaled.reshape(k // 512, 128, 4, n).transpose(0, 1, 3, 2))
    if fmt == "e4m3":
        words = by_word.astype(ml_dtypes.float8_e4m3fn).view(np.uint8)
    else:
        c = by_word.astype(ml_dtypes.float4_e2m1fn).view(np.uint8) & 0xF
        words = (c[..., 0::2] | (c[..., 1::2] << 4)).reshape(k // 512, 128, 2 * n)
    return np.ascontiguousarray(words), np.ascontiguousarray(byte.astype(np.uint8).reshape(k // 512, 16, n))


def unpack_weight(words, scales, fmt):
    g, _, n = scales.shape
    words = np.ascontiguousarray(words).reshape(g, 128, n, -1)
    if fmt == "e4m3":
        vals = words.view(ml_dtypes.float8_e4m3fn).astype(np.float64)
    else:
        nib = np.empty((g, 128, n, 4), np.uint8)
        nib[..., 0::2] = words & 0xF
        nib[..., 1::2] = words >> 4
        vals = E2M1[nib]
    vals = vals * np.repeat(np.exp2(scales.astype(np.float64) - 127.0), 8, axis=1)[..., None]
    return vals.transpose(0, 1, 3, 2).reshape(g * 512, n)


def gelu(v):
    return 0.5 * v * (1.0 + np.tanh(np.sqrt(2.0 / np.pi) * (v + 0.044715 * v**3)))


def bf(x):
    return np.asarray(x, np.float32).astype(ml_dtypes.bfloat16)


def planes(Y):
    n, m = Y.shape
    b = f64(bf(Y)).reshape(n // 32, 32, m)
    amax = np.abs(b).max(1)
    byte = np.clip(np.where(amax > 0, np.frexp(amax)[1] - 1 + 127 - 7, 1), 1, 254)
    codes = (b * np.exp2(127.0 - byte)[:, None, :]).reshape(n, m).astype(np.float32).astype(ml_dtypes.float8_e4m3fn).view(np.uint8)
    words = codes.reshape(n // 512, 128, 4, m).transpose(0, 1, 3, 2)
    return np.ascontiguousarray(words), np.ascontiguousarray(byte.astype(np.uint8).reshape(n // 512, 16, m))


K, T, S, H, N, P = 1024, 4096, 1024, 1536, 512, 512

def setup_inputs():
    n = np.random.standard_normal
    s = mx_kscale(K)[:, None]
    u = mx_kscale(H)[:, None]
    d = {}
    d["tab_words"], d["tab_scales"] = pack_weight(n((K, T)) * s, "e4m3")
    d["offs"] = striped(np.random.permutation(T)[:S])
    d["w1"] = (n((K, H)) * 0.34 / K**0.5 / s).astype(np.float32)
    d["phase"] = np.random.uniform(-1.2, 1.2, (H, S)).astype(np.float32)
    d["gain"] = (np.exp(0.3 * n(H)) * u[:, 0]).astype(np.float32)
    d["w4_words"], d["w4_scales"] = pack_weight(n((H, N)) * 2.2 / H**0.5 / u, "e2m1")
    d["level"] = (0.5 * np.exp(0.8 * n(N))).astype(np.float32)
    d["pos1"] = striped(np.random.permutation(S)[:P])
    d["pos2"] = striped(np.random.permutation(S)[:P])
    return d

def reference(tab_words, tab_scales, offs, w1, phase, gain, w4_words, w4_scales, level, pos1, pos2):
    v = unpack_weight(tab_words, tab_scales, "e4m3")[:, unstriped(offs)]
    w1q = mxq(f64(w1), 0, "e4m3")
    h = np.sin((w1q.T @ v) + f64(phase)) * f64(gain)[:, None]
    hq = mxq(h, 0, "e4m3")
    w4 = unpack_weight(w4_words, w4_scales, "e2m1")
    g2 = np.tanh(w4.T @ hq) * f64(level)[:, None]
    y = np.square(g2[:, unstriped(pos1)]) - g2[:, unstriped(pos2)]
    words, scales = planes(y)
    return y, words, scales

from contextlib import ExitStack

import concourse.mybir as mybir

K, T, S, H, N, PAIRS = 1024, 4096, 1024, 1536, 512, 512
FLOPS = 2 * K * H * S + 2 * H * N * S

F32 = mybir.dt.float32
BF16 = mybir.dt.bfloat16
I32 = mybir.dt.int32
U32 = mybir.dt.uint32
U16 = mybir.dt.uint16
U8 = mybir.dt.uint8
E4M3X4 = mybir.dt.float8_e4m3fn_x4
E2M1X4 = mybir.dt.float4_e2m1fn_x4
ACT = mybir.ActivationFunctionType
ALU = mybir.AluOpType

P = 128
PACK = 4
PASS = P * PACK
K_PASSES = K // PASS
H_PASSES = H // PASS
UNIT = 256
UNITS_PER_BLOCK = S // UNIT
UNITS = H_PASSES * UNITS_PER_BLOCK
HALF = S // 2
QUADS = 4
LAST_PAIRS = 128


def tile_list_rub_buzz_pairs_kernel(
    tc, tab_words, tab_scales, offs, w1, phase, gain, w4_words, w4_scales, level, pos1, pos2, out_0, out_1, out_2
):
    nc = tc.nc
    with ExitStack() as ctx:
        keep = ctx.enter_context(tc.tile_pool(name="keep", bufs=1))
        ring = ctx.enter_context(tc.tile_pool(name="ring", bufs=3))
        psum = ctx.enter_context(tc.psum_pool(name="psum", bufs=1))

        offs_sb = keep.tile([P, S // 16], U16, name="offs_sb")
        pos1_sb = keep.tile([P, PAIRS // 16], U16, name="pos1_sb")
        pos2_sb = keep.tile([P, PAIRS // 16], U16, name="pos2_sb")
        tab_w = [keep.tile([P, T], I32, name=f"tab_w{a}", align_bytes=64) for a in range(K_PASSES)]
        tab_s = keep.tile([P, T], U8, name="tab_s", align_bytes=64)
        v_w = [keep.tile([P, S], U32, name=f"v_w{a}", align_bytes=64) for a in range(K_PASSES)]
        v_s = keep.tile([P, S], U8, name="v_s", align_bytes=64)
        w1_raw = {}
        w1_w = {}
        w1_s = {}
        for b in range(H_PASSES):
            for a in range(K_PASSES):
                w1_raw[b, a] = keep.tile([P, PACK, PASS], F32, name="w1_raw", tag="raw", bufs=4, align_bytes=64)
                w1_w[b, a] = keep.tile([P, PASS], U32, name=f"w1_w{b}{a}", align_bytes=64)
                w1_s[b, a] = keep.tile([P, PASS], U8, name=f"w1_s{b}{a}", align_bytes=64)
        phase_sb = {}
        h_w = {}
        h_s = {}
        for b in range(H_PASSES):
            for half in range(2):
                phase_sb[b, half] = keep.tile([P, PACK, HALF], F32, name="phase_sb", bufs=5, align_bytes=64)
                h_w[b, half] = keep.tile([P, HALF], U32, name=f"h_w{b}{half}", align_bytes=64)
                h_s[b, half] = keep.tile([P, HALF], U8, name=f"h_s{b}{half}", align_bytes=64)
        gain_sb = keep.tile([P, H_PASSES, PACK], F32, name="gain_sb")
        level_sb = keep.tile([P, PACK], F32, name="level_sb")
        w4_w_raw = keep.tile([P, H_PASSES, 2 * N], U8, name="w4_w_raw", align_bytes=64)
        w4_s_raw = keep.tile([P, H_PASSES, N], U8, name="w4_s_raw", align_bytes=64)
        w4_w = keep.tile([P, H_PASSES, 2 * N], U8, name="w4_w", align_bytes=64)
        w4_s = keep.tile([P, H_PASSES, N], U8, name="w4_s", align_bytes=64)

        nc.vector.memset(tab_s[:].bitcast(I32), 0)
        nc.vector.memset(w4_s_raw[:].bitcast(I32), 0)

        def load_table_words(a):
            nc.sync.dma_start(out=tab_w[a][:], in_=tab_words[a].rearrange("p t i -> p (t i)").bitcast(I32))

        def load_w1(b, a):
            rows = w1[a * PASS : (a + 1) * PASS, b * PASS : (b + 1) * PASS]
            nc.sync.dma_start(out=w1_raw[b, a][:], in_=rows.rearrange("(p i) c -> p i c", i=PACK))

        def load_phase(b, lo, hi):
            half = lo // HALF
            rows = phase[b * PASS : (b + 1) * PASS, lo:hi]
            nc.sync.dma_start(
                out=phase_sb[b, half][:, :, lo - half * HALF : hi - half * HALF],
                in_=rows.rearrange("(p t) j -> p t j", t=PACK),
            )

        nc.sync.dma_start(offs_sb[:], offs)
        load_table_words(0)
        for q in range(QUADS):
            nc.gpsimd.dma_start(
                out=tab_s[32 * q : 32 * q + 4 * K_PASSES, :].bitcast(I32),
                in_=tab_scales[:, 4 * q : 4 * q + 4, :].bitcast(I32),
            )
        for q in range(QUADS):
            nc.sync.dma_start(
                out=w4_s_raw[32 * q : 32 * q + 4, :, :].bitcast(I32),
                in_=w4_scales[:, 4 * q : 4 * q + 4, :].rearrange("a r n -> r a n").bitcast(I32),
            )
        load_w1(0, 0)
        load_w1(0, 1)
        load_table_words(1)
        load_phase(0, 0, UNIT)
        nc.sync.dma_start(out=gain_sb[:], in_=gain.rearrange("(b p t) -> p b t", p=P, t=PACK))
        load_phase(0, UNIT, HALF)
        load_w1(1, 0)
        load_phase(0, HALF, S)
        load_w1(1, 1)
        load_phase(1, 0, HALF)
        load_w1(2, 0)
        load_phase(1, HALF, S)
        load_w1(2, 1)
        load_phase(2, 0, HALF)
        nc.sync.dma_start(out=w4_w_raw[:].bitcast(I32), in_=w4_words.rearrange("a p c -> p a c").bitcast(I32))
        load_phase(2, HALF, S)
        nc.sync.dma_start(out=level_sb[:], in_=level.rearrange("(p t) -> p t", t=PACK))
        nc.sync.dma_start(pos1_sb[:], pos1)
        nc.sync.dma_start(pos2_sb[:], pos2)

        def gather_words(a, lo, hi):
            nc.vector.tensor_copy(
                out=v_w[a][:, lo:hi], in_=tab_w[a][:].bitcast(U32).indirect(offs_sb[:, lo // 16 : hi // 16])
            )

        w1_bf = {}

        def round_w1(b, a, part):
            if part == 0:
                w1_bf[b, a] = ring.tile([P, PACK * PASS], BF16, name="w1_bf", bufs=2, align_bytes=64)
            m = slice(part * P // 2, (part + 1) * P // 2)
            nc.scalar.copy(
                out=w1_bf[b, a][:].rearrange("p (t m i) -> p m i t", t=PACK, i=PACK)[:, m],
                in_=w1_raw[b, a][:].rearrange("p i (m t) -> p m i t", t=PACK)[:, m],
            )

        def quantize_w1(b, a):
            nc.vector.quantize_mx(out=w1_w[b, a][:].bitcast(E4M3X4), scales=w1_s[b, a][:], in_=w1_bf[b, a][:])

        gather_words(0, 0, S)
        nc.vector.tensor_copy(out=v_s[:], in_=tab_s[:].indirect(offs_sb[:]))
        for a in range(K_PASSES):
            round_w1(0, a, 0)
            round_w1(0, a, 1)
            quantize_w1(0, a)
        nc.vector.tensor_copy(
            out=w4_s[:].rearrange("p a (t m) -> p a t m", t=PACK),
            in_=w4_s_raw[:].rearrange("p a (m t) -> p a t m", t=PACK),
        )
        gather_words(1, 0, UNIT)

        sines = {}
        h_bf = {}
        args = {}

        def first_stage(u):
            b, q = divmod(u, UNITS_PER_BLOCK)
            half, lo = divmod(q * UNIT, HALF)
            cols = slice(q * UNIT, (q + 1) * UNIT)
            if u == UNITS - 1:
                args[u] = keep.tile([P, PACK, UNIT], F32, name="last_arg", tag="windows", align_bytes=64)
            else:
                args[u] = ring.tile([P, PACK, UNIT], F32, name="arg", align_bytes=64)
            for pair in range(2):
                acc = psum.tile([P, 2, UNIT], F32, name="acc", tag=f"bank{2 * (u % 2) + pair}")
                for e in range(2):
                    t = 2 * pair + e
                    for a in range(K_PASSES):
                        nc.tensor.matmul_mx(
                            out=acc[:, e, :],
                            lhsT=w1_w[b, a][:, t * P : (t + 1) * P].bitcast(E4M3X4),
                            lhsT_scale=w1_s[b, a][:, t * P : (t + 1) * P],
                            rhs=v_w[a][:, cols].bitcast(E4M3X4),
                            rhs_scale=v_s[4 * a :, cols],
                            start=(a == 0),
                            stop=(a == K_PASSES - 1),
                        )
                nc.vector.tensor_tensor(
                    out=args[u][:, 2 * pair : 2 * pair + 2, :],
                    in0=acc[:],
                    in1=phase_sb[b, half][:, 2 * pair : 2 * pair + 2, lo : lo + UNIT],
                    op=ALU.add,
                )
            sines[u] = ring.tile([P, UNIT, PACK], F32, name="sine", align_bytes=64)
            nc.scalar.activation(
                out=sines[u][:].rearrange("p (c i) t -> p c t i", i=4),
                in_=args[u][:].rearrange("p t (c i) -> p c t i", i=4),
                func=ACT.Sin,
            )

        def apply_gain(u):
            b = u // UNITS_PER_BLOCK
            h_bf[u] = ring.tile([P, UNIT, PACK], BF16, name="h_bf", align_bytes=64)
            nc.vector.tensor_tensor(
                out=h_bf[u][:],
                in0=sines[u][:],
                in1=gain_sb[:, b, :].unsqueeze(1).to_broadcast([P, UNIT, PACK]),
                op=ALU.mult,
            )

        def quantize_h(u):
            b, q = divmod(u, UNITS_PER_BLOCK)
            half, lo = divmod(q * UNIT, HALF)
            nc.vector.quantize_mx(
                out=h_w[b, half][:, lo : lo + UNIT].bitcast(E4M3X4),
                scales=h_s[b, half][:, lo : lo + UNIT],
                in_=h_bf[u][:].rearrange("p j t -> p (j t)"),
            )

        z = {}

        def second_pass(half, t, b, lo, hi, start, stop):
            nc.tensor.matmul_mx(
                out=z[half, t][:, lo:hi],
                lhsT=w4_w[:, b, 2 * t * P : 2 * (t + 1) * P].bitcast(E2M1X4),
                lhsT_scale=w4_s[:, b, t * P : (t + 1) * P],
                rhs=h_w[b, half][:, lo:hi].bitcast(E4M3X4),
                rhs_scale=h_s[b, half][:, lo:hi],
                start=start,
                stop=stop,
            )

        for u in range(UNITS + 2):
            b, q = divmod(u, UNITS_PER_BLOCK)
            if u < UNITS:
                first_stage(u)
            if u == 0:
                gather_words(1, UNIT, HALF)
            if u == 1:
                gather_words(1, HALF, S)
            if 1 <= u <= UNITS:
                apply_gain(u - 1)
            if u >= 2:
                quantize_h(u - 2)
            if b + 1 < H_PASSES:
                round_w1(b + 1, q // 2, q % 2)
                if q % 2 == 1:
                    quantize_w1(b + 1, q // 2)
            if b == H_PASSES - 1 and q < H_PASSES:
                nc.scalar.copy(
                    out=w4_w[:, q, :].bitcast(U16).rearrange("p (t m) -> p m t", t=PACK),
                    in_=w4_w_raw[:, q, :].bitcast(U16).rearrange("p (m t) -> p m t", t=PACK),
                )
            if u == UNITS - 1:
                for t in range(PACK):
                    z[0, t] = psum.tile([P, HALF], F32, name="z_first", tag=f"bank{4 + t}")
                    for bb in range(H_PASSES):
                        second_pass(0, t, bb, 0, HALF, bb == 0, bb == H_PASSES - 1)
            if u == UNITS:
                for t in range(PACK):
                    z[1, t] = psum.tile([P, HALF], F32, name="z_second", tag=f"bank{t}")
                    for bb in range(H_PASSES - 1):
                        second_pass(1, t, bb, 0, HALF, bb == 0, False)
                    second_pass(1, t, H_PASSES - 1, 0, UNIT, False, False)
        for t in range(PACK):
            second_pass(1, t, H_PASSES - 1, UNIT, HALF, False, True)

        windows = keep.tile([P, PACK, S], F32, name="windows", tag="windows", align_bytes=64)
        y = keep.tile([P, PACK, PAIRS], F32, name="y", tag="raw", bufs=4, align_bytes=64)
        y_w = keep.tile([P, PAIRS], U32, name="y_w", align_bytes=64)
        y_s = keep.tile([P, PAIRS], U8, name="y_s", align_bytes=64)

        def bound(t):
            for half in range(2):
                nc.scalar.activation(
                    out=windows[:, t, half * HALF : (half + 1) * HALF], in_=z[half, t][:], func=ACT.Tanh, scale=-1.0
                )

        bound(0)
        out_rows = out_0.rearrange("(p t) m -> p t m", t=PACK)
        out_words = out_1[0].rearrange("p m t -> p (m t)").bitcast(I32)
        for part, (lo, hi) in enumerate(((0, PAIRS - LAST_PAIRS), (PAIRS - LAST_PAIRS, PAIRS))):
            piece = hi - lo
            m = slice(lo, hi)
            lists = slice(lo // 16, hi // 16)
            squares = {}
            seconds = {}
            for t in range(PACK + 1):
                if t < PACK:
                    first = ring.tile([P, piece], F32, name="first")
                    seconds[t] = ring.tile([P, piece], F32, name="second")
                    squares[t] = ring.tile([P, piece], F32, name="square")
                    nc.vector.tensor_copy(out=first[:], in_=windows[:, t, :].indirect(pos1_sb[:, lists]))
                    if part == 0 and t + 1 < PACK:
                        bound(t + 1)
                    nc.scalar.activation(
                        out=squares[t][:], in_=first[:], func=ACT.Square, scale=level_sb[:, t : t + 1]
                    )
                    nc.vector.tensor_copy(out=seconds[t][:], in_=windows[:, t, :].indirect(pos2_sb[:, lists]))
                if t >= 1:
                    nc.vector.scalar_tensor_tensor(
                        out=y[:, t - 1, m],
                        in0=seconds[t - 1][:],
                        scalar=level_sb[:, t - 1 : t],
                        in1=squares[t - 1][:],
                        op0=ALU.mult,
                        op1=ALU.add,
                    )
                if t in (2, 4):
                    nc.sync.dma_start(out=out_rows[:, t - 2 : t, m], in_=y[:, t - 2 : t, m])
            y_bf = ring.tile([P, piece, PACK], BF16, name="y_bf", bufs=2, align_bytes=64)
            rounder = nc.scalar.copy if part == 0 else nc.vector.tensor_copy
            rounder(
                out=y_bf[:].rearrange("p (c i) t -> p c t i", i=4),
                in_=y[:, :, m].rearrange("p t (c i) -> p c t i", i=4),
            )
            nc.vector.quantize_mx(
                out=y_w[:, m].bitcast(E4M3X4), scales=y_s[:, m], in_=y_bf[:].rearrange("p j t -> p (j t)")
            )
            nc.sync.dma_start(out=out_words[:, m], in_=y_w[:, m].bitcast(I32))
        for q in range(QUADS):
            queue = nc.scalar if q % 2 == 0 else nc.sync
            queue.dma_start(out=out_2[0, 4 * q : 4 * q + 4, :].bitcast(I32), in_=y_s[32 * q : 32 * q + 4, :].bitcast(I32))
